import numpy as np
import ml_dtypes

BF16 = ml_dtypes.bfloat16


def bf(x):
    return np.asarray(x, np.float32).astype(BF16)


def f32(x):
    return np.asarray(x, np.float32)


def f64(x):
    return np.asarray(x).astype(np.float64)


def striped(idx):
    return np.tile(idx.reshape(-1, 16).T, (8, 1))


S, K, M, N, D, V = 1024, 128, 512, 128, 4, 32


def gelu_tanh(v):
    return 0.5 * v * (1.0 + np.tanh(np.sqrt(2.0 / np.pi) * (v + 0.044715 * v**3)))


def setup_inputs():
    return {"table": bf(np.random.standard_normal((S, K))), "w": bf(np.random.standard_normal((K, M)) / np.sqrt(K)), "b": f32(0.5 * np.random.standard_normal((M, 1))), "offs": striped(np.random.permutation(S)[:N])}


def reference(table, w, b, offs):
    idx = offs[:16].T.reshape(-1)
    x = f64(table)[idx].T
    y = f64(w).T @ x
    z = gelu_tanh(y + f64(b))
    return z.reshape(M, V, D).max(axis=2)

@@ -1,0 +1,66 @@
+import concourse.mybir as mybir
+from concourse.masks import make_identity
+
+P = 128
+S, K, M, N, D = 1024, 128, 512, 128, 4
+NODE_BLOCKS = S // P
+OUT_BLOCKS = M // P
+HALF = S // 2
+
+FLOPS = 2 * K * M * N
+
+BF16, F32, U16 = mybir.dt.bfloat16, mybir.dt.float32, mybir.dt.uint16
+GELU = mybir.ActivationFunctionType.Gelu_apprx_tanh
+
+
+def tile_gather_matmul_kernel(tc, table, w, b, offs, out):
+    nc = tc.nc
+    with (
+        tc.tile_pool(name="held", bufs=1) as held,
+        tc.psum_pool(name="flip", bufs=2) as flip,
+        tc.psum_pool(name="prod", bufs=OUT_BLOCKS) as prod,
+    ):
+        offsets = held.tile([P, N // 16], U16, name="offsets")
+        nc.sync.dma_start(offsets[:], offs)
+        rows = held.tile([P, NODE_BLOCKS, K], BF16, name="rows")
+        nc.sync.dma_start(rows[:], table.rearrange("(c p) k -> p c k", p=P))
+        weights = held.tile([K, M], BF16, name="weights")
+        nc.scalar.dma_start(weights[:], w)
+        bias = held.tile([P, OUT_BLOCKS], F32, name="bias")
+        with nc.allow_non_contiguous_dma(reason="one float32 bias value to a partition"):
+            nc.scalar.dma_start(bias[:], b.rearrange("(a p) o -> p (a o)", p=P))
+
+        identity = held.tile([P, P], BF16, name="identity")
+        make_identity(nc, identity[:])
+
+        table_t = held.tile([K, S], BF16, name="table_t")
+        for h in range(S // HALF):
+            flipped = flip.tile([K, HALF], BF16, name="flipped")
+            for j in range(HALF // P):
+                c = h * (HALF // P) + j
+                nc.tensor.transpose(flipped[:, j * P : (j + 1) * P], rows[:, c, :], identity[:])
+            nc.vector.tensor_copy(table_t[:, h * HALF : (h + 1) * HALF], flipped[:])
+
+        z = held.tile([P, OUT_BLOCKS * N], F32, name="z")
+        for a in range(OUT_BLOCKS):
+            product = prod.tile([P, N], F32, name="product")
+            nc.tensor.matmul(
+                product[:],
+                weights[:, a * P : (a + 1) * P],
+                table_t[:].indirect(offsets[:]),
+                start=True,
+                stop=True,
+            )
+            nc.scalar.activation(z[:, a * N : (a + 1) * N], product[:], GELU, bias=bias[:, a : a + 1])
+
+        pooled = held.tile([P, OUT_BLOCKS * (N // D)], F32, name="pooled")
+        nc.vector.tensor_reduce(
+            pooled[:],
+            z[:].rearrange("p (g t) -> p g t", t=D),
+            axis=mybir.AxisListType.X,
+            op=mybir.AluOpType.max,
+        )
+        nc.sync.dma_start(
+            out.rearrange("(a p) v -> p a v", p=P),
+            pooled[:].rearrange("p (a v) -> p a v", a=OUT_BLOCKS),
+        )

@@ -3,9 +3,11 @@ from concourse.masks import make_identity
 
 P = 128
 S, K, M, N, D = 1024, 128, 512, 128, 4
-NODE_BLOCKS = S // P
+V = N // D
 OUT_BLOCKS = M // P
-HALF = S // 2
+PIECE_BLOCKS = (2, 2, 2, 1, 1)
+FLIP_BANKS = 4
+assert sum(PIECE_BLOCKS) * P == S
 
 FLOPS = 2 * K * M * N
 
@@ -17,31 +19,46 @@ def tile_gather_matmul_kernel(tc, table, w, b, offs, out):
     nc = tc.nc
     with (
         tc.tile_pool(name="held", bufs=1) as held,
-        tc.psum_pool(name="flip", bufs=2) as flip,
+        tc.tile_pool(name="work", bufs=OUT_BLOCKS) as work,
+        tc.psum_pool(name="flip", bufs=FLIP_BANKS) as flip,
         tc.psum_pool(name="prod", bufs=OUT_BLOCKS) as prod,
     ):
         offsets = held.tile([P, N // 16], U16, name="offsets")
         nc.sync.dma_start(offsets[:], offs)
-        rows = held.tile([P, NODE_BLOCKS, K], BF16, name="rows")
-        nc.sync.dma_start(rows[:], table.rearrange("(c p) k -> p c k", p=P))
+        rows = []
+        first_nodes = []
+        node = 0
+        for q, blocks in enumerate(PIECE_BLOCKS):
+            piece_rows = held.tile([P, blocks, K], BF16, name="rows%d" % q)
+            queue = nc.sync if q % 2 == 0 else nc.scalar
+            queue.dma_start(piece_rows[:], table[node : node + blocks * P, :].rearrange("(c p) k -> p c k", p=P))
+            rows.append(piece_rows)
+            first_nodes.append(node)
+            node += blocks * P
+
+        identity = held.tile([P, P], BF16, name="identity")
+        make_identity(nc, identity[:])
         weights = held.tile([K, M], BF16, name="weights")
-        nc.scalar.dma_start(weights[:], w)
+        nc.sync.dma_start(weights[:], w)
         bias = held.tile([P, OUT_BLOCKS], F32, name="bias")
         with nc.allow_non_contiguous_dma(reason="one float32 bias value to a partition"):
             nc.scalar.dma_start(bias[:], b.rearrange("(a p) o -> p (a o)", p=P))
 
-        identity = held.tile([P, P], BF16, name="identity")
-        make_identity(nc, identity[:])
+        warm = held.tile([P, 1], F32, name="warm")
+        nc.vector.memset(warm[:], 0.0)
+        nc.scalar.activation(warm[:], warm[:], GELU)
 
         table_t = held.tile([K, S], BF16, name="table_t")
-        for h in range(S // HALF):
-            flipped = flip.tile([K, HALF], BF16, name="flipped")
-            for j in range(HALF // P):
-                c = h * (HALF // P) + j
-                nc.tensor.transpose(flipped[:, j * P : (j + 1) * P], rows[:, c, :], identity[:])
-            nc.vector.tensor_copy(table_t[:, h * HALF : (h + 1) * HALF], flipped[:])
+        for q, blocks in enumerate(PIECE_BLOCKS):
+            flipped = flip.tile([K, blocks * P], BF16, name="flipped")
+            for c in range(blocks):
+                nc.tensor.transpose(flipped[:, c * P : (c + 1) * P], rows[q][:, c, :], identity[:])
+            piece_columns = table_t[:, first_nodes[q] : first_nodes[q] + blocks * P]
+            if q % 2 == 0:
+                nc.vector.tensor_copy(piece_columns, flipped[:])
+            else:
+                nc.scalar.copy(piece_columns, flipped[:])
 
-        z = held.tile([P, OUT_BLOCKS * N], F32, name="z")
         for a in range(OUT_BLOCKS):
             product = prod.tile([P, N], F32, name="product")
             nc.tensor.matmul(
@@ -51,16 +68,13 @@ def tile_gather_matmul_kernel(tc, table, w, b, offs, out):
                 start=True,
                 stop=True,
             )
-            nc.scalar.activation(z[:, a * N : (a + 1) * N], product[:], GELU, bias=bias[:, a : a + 1])
-
-        pooled = held.tile([P, OUT_BLOCKS * (N // D)], F32, name="pooled")
-        nc.vector.tensor_reduce(
-            pooled[:],
-            z[:].rearrange("p (g t) -> p g t", t=D),
-            axis=mybir.AxisListType.X,
-            op=mybir.AluOpType.max,
-        )
-        nc.sync.dma_start(
-            out.rearrange("(a p) v -> p a v", p=P),
-            pooled[:].rearrange("p (a v) -> p a v", a=OUT_BLOCKS),
-        )
+            z = work.tile([P, N], F32, name="z")
+            nc.scalar.activation(z[:], product[:], GELU, bias=bias[:, a : a + 1])
+            pooled = work.tile([P, V], F32, name="pooled")
+            nc.vector.tensor_reduce(
+                pooled[:],
+                z[:].rearrange("p (v t) -> p v t", t=D),
+                axis=mybir.AxisListType.X,
+                op=mybir.AluOpType.max,
+            )
+            nc.sync.dma_start(out[a * P : (a + 1) * P, :], pooled[:])

@@ -5,7 +5,7 @@ P = 128
 S, K, M, N, D = 1024, 128, 512, 128, 4
 V = N // D
 OUT_BLOCKS = M // P
-PIECE_BLOCKS = (2, 2, 2, 1, 1)
+PIECE_BLOCKS = (1, 2, 2, 2, 1)
 FLIP_BANKS = 4
 assert sum(PIECE_BLOCKS) * P == S
 
@@ -23,8 +23,6 @@ def tile_gather_matmul_kernel(tc, table, w, b, offs, out):
         tc.psum_pool(name="flip", bufs=FLIP_BANKS) as flip,
         tc.psum_pool(name="prod", bufs=OUT_BLOCKS) as prod,
     ):
-        offsets = held.tile([P, N // 16], U16, name="offsets")
-        nc.sync.dma_start(offsets[:], offs)
         rows = []
         first_nodes = []
         node = 0
@@ -38,11 +36,13 @@ def tile_gather_matmul_kernel(tc, table, w, b, offs, out):
 
         identity = held.tile([P, P], BF16, name="identity")
         make_identity(nc, identity[:])
+        offsets = held.tile([P, N // 16], U16, name="offsets")
+        nc.sync.dma_start(offsets[:], offs)
         weights = held.tile([K, M], BF16, name="weights")
         nc.sync.dma_start(weights[:], w)
         bias = held.tile([P, OUT_BLOCKS], F32, name="bias")
         with nc.allow_non_contiguous_dma(reason="one float32 bias value to a partition"):
-            nc.scalar.dma_start(bias[:], b.rearrange("(a p) o -> p (a o)", p=P))
+            nc.sync.dma_start(bias[:], b.rearrange("(a p) o -> p (a o)", p=P))
 
         warm = held.tile([P, 1], F32, name="warm")
         nc.vector.memset(warm[:], 0.0)

@@ -6,7 +6,9 @@ S, K, M, N, D = 1024, 128, 512, 128, 4
 V = N // D
 OUT_BLOCKS = M // P
 PIECE_BLOCKS = (1, 2, 2, 2, 1)
-FLIP_BANKS = 4
+FLIP_BANKS = 3
+WARM_COLUMNS = 512
+WARM_MATMULS = 5
 assert sum(PIECE_BLOCKS) * P == S
 
 FLOPS = 2 * K * M * N
@@ -20,6 +22,7 @@ def tile_gather_matmul_kernel(tc, table, w, b, offs, out):
     with (
         tc.tile_pool(name="held", bufs=1) as held,
         tc.tile_pool(name="work", bufs=OUT_BLOCKS) as work,
+        tc.psum_pool(name="idle", bufs=1) as idle,
         tc.psum_pool(name="flip", bufs=FLIP_BANKS) as flip,
         tc.psum_pool(name="prod", bufs=OUT_BLOCKS) as prod,
     ):
@@ -47,6 +50,12 @@ def tile_gather_matmul_kernel(tc, table, w, b, offs, out):
         warm = held.tile([P, 1], F32, name="warm")
         nc.vector.memset(warm[:], 0.0)
         nc.scalar.activation(warm[:], warm[:], GELU)
+
+        zeros = held.tile([P, WARM_COLUMNS], BF16, name="zeros")
+        nc.vector.memset(zeros[:], 0.0)
+        unused = idle.tile([P, WARM_COLUMNS], F32, name="unused")
+        for i in range(WARM_MATMULS):
+            nc.tensor.matmul(unused[:], zeros[:, 0:P], zeros[:], start=True, stop=True)
 
         table_t = held.tile([K, S], BF16, name="table_t")
         for q, blocks in enumerate(PIECE_BLOCKS):

@@ -6,9 +6,7 @@ S, K, M, N, D = 1024, 128, 512, 128, 4
 V = N // D
 OUT_BLOCKS = M // P
 PIECE_BLOCKS = (1, 2, 2, 2, 1)
-FLIP_BANKS = 3
-WARM_COLUMNS = 512
-WARM_MATMULS = 5
+FLIP_BANKS = 4
 assert sum(PIECE_BLOCKS) * P == S
 
 FLOPS = 2 * K * M * N
@@ -22,7 +20,6 @@ def tile_gather_matmul_kernel(tc, table, w, b, offs, out):
     with (
         tc.tile_pool(name="held", bufs=1) as held,
         tc.tile_pool(name="work", bufs=OUT_BLOCKS) as work,
-        tc.psum_pool(name="idle", bufs=1) as idle,
         tc.psum_pool(name="flip", bufs=FLIP_BANKS) as flip,
         tc.psum_pool(name="prod", bufs=OUT_BLOCKS) as prod,
     ):
@@ -32,7 +29,7 @@ def tile_gather_matmul_kernel(tc, table, w, b, offs, out):
         for q, blocks in enumerate(PIECE_BLOCKS):
             piece_rows = held.tile([P, blocks, K], BF16, name="rows%d" % q)
             queue = nc.sync if q % 2 == 0 else nc.scalar
-            queue.dma_start(piece_rows[:], table[node : node + blocks * P, :].rearrange("(c p) k -> p c k", p=P))
+            queue.dma_start(piece_rows[:], table[node : node + blocks * P, :].rearrange("(p c) k -> p c k", p=P))
             rows.append(piece_rows)
             first_nodes.append(node)
             node += blocks * P
@@ -51,22 +48,16 @@ def tile_gather_matmul_kernel(tc, table, w, b, offs, out):
         nc.vector.memset(warm[:], 0.0)
         nc.scalar.activation(warm[:], warm[:], GELU)
 
-        zeros = held.tile([P, WARM_COLUMNS], BF16, name="zeros")
-        nc.vector.memset(zeros[:], 0.0)
-        unused = idle.tile([P, WARM_COLUMNS], F32, name="unused")
-        for i in range(WARM_MATMULS):
-            nc.tensor.matmul(unused[:], zeros[:, 0:P], zeros[:], start=True, stop=True)
-
         table_t = held.tile([K, S], BF16, name="table_t")
         for q, blocks in enumerate(PIECE_BLOCKS):
-            flipped = flip.tile([K, blocks * P], BF16, name="flipped")
+            flipped = flip.tile([K, blocks, P], BF16, name="flipped")
             for c in range(blocks):
-                nc.tensor.transpose(flipped[:, c * P : (c + 1) * P], rows[q][:, c, :], identity[:])
-            piece_columns = table_t[:, first_nodes[q] : first_nodes[q] + blocks * P]
+                nc.tensor.transpose(flipped[:, c, :], rows[q][:, c, :], identity[:])
+            piece_columns = table_t[:, first_nodes[q] : first_nodes[q] + blocks * P].rearrange("k (p c) -> k p c", c=blocks)
             if q % 2 == 0:
-                nc.vector.tensor_copy(piece_columns, flipped[:])
+                nc.vector.tensor_copy(piece_columns, flipped[:].rearrange("k c p -> k p c"))
             else:
-                nc.scalar.copy(piece_columns, flipped[:])
+                nc.scalar.copy(piece_columns, flipped[:].rearrange("k c p -> k p c"))
 
         for a in range(OUT_BLOCKS):
             product = prod.tile([P, N], F32, name="product")

@@ -7,6 +7,7 @@ V = N // D
 OUT_BLOCKS = M // P
 PIECE_BLOCKS = (1, 2, 2, 2, 1)
 FLIP_BANKS = 4
+WARM_MATMULS = 12
 assert sum(PIECE_BLOCKS) * P == S
 
 FLOPS = 2 * K * M * N
@@ -23,6 +24,12 @@ def tile_gather_matmul_kernel(tc, table, w, b, offs, out):
         tc.psum_pool(name="flip", bufs=FLIP_BANKS) as flip,
         tc.psum_pool(name="prod", bufs=OUT_BLOCKS) as prod,
     ):
+        zeros = held.tile([P, P], BF16, name="zeros")
+        nc.gpsimd.memset(zeros[:], 0.0)
+        unread = prod.tile([P, N], F32, name="unread", tag="product")
+        for i in range(WARM_MATMULS):
+            nc.tensor.matmul(unread[:], zeros[:], zeros[:], start=True, stop=True)
+
         rows = []
         first_nodes = []
         node = 0

@@ -6,8 +6,10 @@ S, K, M, N, D = 1024, 128, 512, 128, 4
 V = N // D
 OUT_BLOCKS = M // P
 PIECE_BLOCKS = (1, 2, 2, 2, 1)
-FLIP_BANKS = 4
+SINGLES_FROM = 3
+PSUM_BANKS = 8
 WARM_MATMULS = 12
+WAIT_COLUMNS = 16
 assert sum(PIECE_BLOCKS) * P == S
 
 FLOPS = 2 * K * M * N
@@ -21,12 +23,11 @@ def tile_gather_matmul_kernel(tc, table, w, b, offs, out):
     with (
         tc.tile_pool(name="held", bufs=1) as held,
         tc.tile_pool(name="work", bufs=OUT_BLOCKS) as work,
-        tc.psum_pool(name="flip", bufs=FLIP_BANKS) as flip,
-        tc.psum_pool(name="prod", bufs=OUT_BLOCKS) as prod,
+        tc.psum_pool(name="psum", bufs=PSUM_BANKS) as psum,
     ):
         zeros = held.tile([P, P], BF16, name="zeros")
         nc.gpsimd.memset(zeros[:], 0.0)
-        unread = prod.tile([P, N], F32, name="unread", tag="product")
+        unread = psum.tile([P, N], F32, name="unread", tag="bank")
         for i in range(WARM_MATMULS):
             nc.tensor.matmul(unread[:], zeros[:], zeros[:], start=True, stop=True)
 
@@ -34,9 +35,10 @@ def tile_gather_matmul_kernel(tc, table, w, b, offs, out):
         first_nodes = []
         node = 0
         for q, blocks in enumerate(PIECE_BLOCKS):
+            order = "(p c) k -> p c k" if q < SINGLES_FROM else "(c p) k -> p c k"
             piece_rows = held.tile([P, blocks, K], BF16, name="rows%d" % q)
             queue = nc.sync if q % 2 == 0 else nc.scalar
-            queue.dma_start(piece_rows[:], table[node : node + blocks * P, :].rearrange("(p c) k -> p c k", p=P))
+            queue.dma_start(piece_rows[:], table[node : node + blocks * P, :].rearrange(order, p=P))
             rows.append(piece_rows)
             first_nodes.append(node)
             node += blocks * P
@@ -56,18 +58,26 @@ def tile_gather_matmul_kernel(tc, table, w, b, offs, out):
         nc.scalar.activation(warm[:], warm[:], GELU)
 
         table_t = held.tile([K, S], BF16, name="table_t")
+        copies = 0
         for q, blocks in enumerate(PIECE_BLOCKS):
-            flipped = flip.tile([K, blocks, P], BF16, name="flipped")
-            for c in range(blocks):
-                nc.tensor.transpose(flipped[:, c, :], rows[q][:, c, :], identity[:])
-            piece_columns = table_t[:, first_nodes[q] : first_nodes[q] + blocks * P].rearrange("k (p c) -> k p c", c=blocks)
-            if q % 2 == 0:
-                nc.vector.tensor_copy(piece_columns, flipped[:].rearrange("k c p -> k p c"))
-            else:
-                nc.scalar.copy(piece_columns, flipped[:].rearrange("k c p -> k p c"))
+            together = blocks if q < SINGLES_FROM else 1
+            for first in range(0, blocks, together):
+                flipped = psum.tile([K, together, P], BF16, name="flipped", tag="bank")
+                for c in range(together):
+                    nc.tensor.transpose(flipped[:, c, :], rows[q][:, first + c, :], identity[:])
+                node = first_nodes[q] + first * P
+                columns = table_t[:, node : node + together * P].rearrange("k (p c) -> k p c", c=together)
+                if copies % 2 == 0:
+                    nc.scalar.copy(columns, flipped[:].rearrange("k c p -> k p c"))
+                else:
+                    nc.vector.tensor_copy(columns, flipped[:].rearrange("k c p -> k p c"))
+                copies += 1
+
+        middle = first_nodes[len(PIECE_BLOCKS) // 2]
+        nc.tensor.matmul(unread[:, 0:WAIT_COLUMNS], weights[:, 0:P], table_t[:, middle : middle + WAIT_COLUMNS], start=True, stop=True)
 
         for a in range(OUT_BLOCKS):
-            product = prod.tile([P, N], F32, name="product")
+            product = psum.tile([P, N], F32, name="product", tag="bank")
             nc.tensor.matmul(
                 product[:],
                 weights[:, a * P : (a + 1) * P],

@@ -8,7 +8,8 @@ OUT_BLOCKS = M // P
 PIECE_BLOCKS = (1, 2, 2, 2, 1)
 SINGLES_FROM = 3
 PSUM_BANKS = 8
-WARM_MATMULS = 12
+WARM_MATMULS = 3
+WARM_COLUMNS = 512
 WAIT_COLUMNS = 16
 assert sum(PIECE_BLOCKS) * P == S
 
@@ -27,9 +28,9 @@ def tile_gather_matmul_kernel(tc, table, w, b, offs, out):
     ):
         zeros = held.tile([P, P], BF16, name="zeros")
         nc.gpsimd.memset(zeros[:], 0.0)
-        unread = psum.tile([P, N], F32, name="unread", tag="bank")
+        unread = psum.tile([P, WARM_COLUMNS], F32, name="unread", tag="bank")
         for i in range(WARM_MATMULS):
-            nc.tensor.matmul(unread[:], zeros[:], zeros[:], start=True, stop=True)
+            nc.tensor.matmul(unread[:], zeros[:], zeros[:, 0:1].to_broadcast([P, WARM_COLUMNS]), start=True, stop=True)
 
         rows = []
         first_nodes = []
@@ -58,7 +59,6 @@ def tile_gather_matmul_kernel(tc, table, w, b, offs, out):
         nc.scalar.activation(warm[:], warm[:], GELU)
 
         table_t = held.tile([K, S], BF16, name="table_t")
-        copies = 0
         for q, blocks in enumerate(PIECE_BLOCKS):
             together = blocks if q < SINGLES_FROM else 1
             for first in range(0, blocks, together):
@@ -67,11 +67,10 @@ def tile_gather_matmul_kernel(tc, table, w, b, offs, out):
                     nc.tensor.transpose(flipped[:, c, :], rows[q][:, first + c, :], identity[:])
                 node = first_nodes[q] + first * P
                 columns = table_t[:, node : node + together * P].rearrange("k (p c) -> k p c", c=together)
-                if copies % 2 == 0:
+                if q < SINGLES_FROM and q % 2 == 0:
                     nc.scalar.copy(columns, flipped[:].rearrange("k c p -> k p c"))
                 else:
                     nc.vector.tensor_copy(columns, flipped[:].rearrange("k c p -> k p c"))
-                copies += 1
 
         middle = first_nodes[len(PIECE_BLOCKS) // 2]
         nc.tensor.matmul(unread[:, 0:WAIT_COLUMNS], weights[:, 0:P], table_t[:, middle : middle + WAIT_COLUMNS], start=True, stop=True)

import concourse.mybir as mybir
from concourse.masks import make_identity

P = 128
S, K, M, N, D = 1024, 128, 512, 128, 4
V = N // D
OUT_BLOCKS = M // P
PIECE_BLOCKS = (1, 2, 2, 2, 1)
SINGLES_FROM = 3
PSUM_BANKS = 8
WARM_MATMULS = 3
WARM_COLUMNS = 512
WAIT_COLUMNS = 16
assert sum(PIECE_BLOCKS) * P == S

FLOPS = 2 * K * M * N

BF16, F32, U16 = mybir.dt.bfloat16, mybir.dt.float32, mybir.dt.uint16
GELU = mybir.ActivationFunctionType.Gelu_apprx_tanh


def tile_gather_matmul_kernel(tc, table, w, b, offs, out):
    nc = tc.nc
    with (
        tc.tile_pool(name="held", bufs=1) as held,
        tc.tile_pool(name="work", bufs=OUT_BLOCKS) as work,
        tc.psum_pool(name="psum", bufs=PSUM_BANKS) as psum,
    ):
        zeros = held.tile([P, P], BF16, name="zeros")
        nc.gpsimd.memset(zeros[:], 0.0)
        unread = psum.tile([P, WARM_COLUMNS], F32, name="unread", tag="bank")
        for i in range(WARM_MATMULS):
            nc.tensor.matmul(unread[:], zeros[:], zeros[:, 0:1].to_broadcast([P, WARM_COLUMNS]), start=True, stop=True)

        rows = []
        first_nodes = []
        node = 0
        for q, blocks in enumerate(PIECE_BLOCKS):
            order = "(p c) k -> p c k" if q < SINGLES_FROM else "(c p) k -> p c k"
            piece_rows = held.tile([P, blocks, K], BF16, name="rows%d" % q)
            queue = nc.sync if q % 2 == 0 else nc.scalar
            queue.dma_start(piece_rows[:], table[node : node + blocks * P, :].rearrange(order, p=P))
            rows.append(piece_rows)
            first_nodes.append(node)
            node += blocks * P

        identity = held.tile([P, P], BF16, name="identity")
        make_identity(nc, identity[:])
        offsets = held.tile([P, N // 16], U16, name="offsets")
        nc.sync.dma_start(offsets[:], offs)
        weights = held.tile([K, M], BF16, name="weights")
        nc.sync.dma_start(weights[:], w)
        bias = held.tile([P, OUT_BLOCKS], F32, name="bias")
        with nc.allow_non_contiguous_dma(reason="one float32 bias value to a partition"):
            nc.sync.dma_start(bias[:], b.rearrange("(a p) o -> p (a o)", p=P))

        warm = held.tile([P, 1], F32, name="warm")
        nc.vector.memset(warm[:], 0.0)
        nc.scalar.activation(warm[:], warm[:], GELU)

        table_t = held.tile([K, S], BF16, name="table_t")
        for q, blocks in enumerate(PIECE_BLOCKS):
            together = blocks if q < SINGLES_FROM else 1
            for first in range(0, blocks, together):
                flipped = psum.tile([K, together, P], BF16, name="flipped", tag="bank")
                for c in range(together):
                    nc.tensor.transpose(flipped[:, c, :], rows[q][:, first + c, :], identity[:])
                node = first_nodes[q] + first * P
                columns = table_t[:, node : node + together * P].rearrange("k (p c) -> k p c", c=together)
                if q < SINGLES_FROM and q % 2 == 0:
                    nc.scalar.copy(columns, flipped[:].rearrange("k c p -> k p c"))
                else:
                    nc.vector.tensor_copy(columns, flipped[:].rearrange("k c p -> k p c"))

        middle = first_nodes[len(PIECE_BLOCKS) // 2]
        nc.tensor.matmul(unread[:, 0:WAIT_COLUMNS], weights[:, 0:P], table_t[:, middle : middle + WAIT_COLUMNS], start=True, stop=True)

        for a in range(OUT_BLOCKS):
            product = psum.tile([P, N], F32, name="product", tag="bank")
            nc.tensor.matmul(
                product[:],
                weights[:, a * P : (a + 1) * P],
                table_t[:].indirect(offsets[:]),
                start=True,
                stop=True,
            )
            z = work.tile([P, N], F32, name="z")
            nc.scalar.activation(z[:], product[:], GELU, bias=bias[:, a : a + 1])
            pooled = work.tile([P, V], F32, name="pooled")
            nc.vector.tensor_reduce(
                pooled[:],
                z[:].rearrange("p (v t) -> p v t", t=D),
                axis=mybir.AxisListType.X,
                op=mybir.AluOpType.max,
            )
            nc.sync.dma_start(out[a * P : (a + 1) * P, :], pooled[:])
